import numpy as np
import ml_dtypes


def mxq(x, axis, fmt="e4m3"):
    dtype, down = {"e4m3": (ml_dtypes.float8_e4m3fn, 7), "e5m2": (ml_dtypes.float8_e5m2, 14)}[fmt]
    v = np.moveaxis(np.asarray(x, np.float32).astype(ml_dtypes.bfloat16).astype(np.float64), axis, -1)
    blocks = v.reshape(v.shape[:-1] + (-1, 32))
    amax = np.abs(blocks).max(-1, keepdims=True)
    byte = np.maximum(np.where(amax > 0, np.frexp(amax)[1] - 1 + 127, 0) - down, 1)
    scale = np.exp2(byte - 127.0)
    codes = (blocks / scale).astype(np.float32).astype(dtype).astype(np.float64)
    return np.moveaxis((codes * scale).reshape(v.shape), -1, axis)


WIDE = False


def mx_kscale(k):
    if not WIDE:
        return np.ones(k)
    levels = np.array([10, -10, 5, -5, 0])
    if k % 512:
        return np.exp2(np.random.permutation(np.resize(levels, k // 32))).repeat(32)
    a = np.empty((k // 512, 16))
    for p in range(k // 512):
        a[p, :8] = np.random.permutation(np.resize(levels, 8))
        for g in range(8):
            far = levels[np.abs(levels - a[p, g]) >= 10]
            a[p, g + 8] = far[np.random.randint(len(far))]
    return np.exp2(a.ravel()).repeat(32)


def f64(x):
    return np.asarray(x).astype(np.float64)


def striped(idx):
    return np.tile(np.asarray(idx).reshape(-1, 16).T, (8, 1)).astype(np.uint16)


def unstriped(offs):
    return offs[:16].T.reshape(-1).astype(np.int64)


def striped8(idx):
    return np.asarray(idx).reshape(8, -1, 16).transpose(0, 2, 1).reshape(128, -1).astype(np.uint16)


def unstriped8(offs):
    return offs.reshape(8, 16, -1).transpose(0, 2, 1).reshape(8, -1).astype(np.int64)


def pick8(x, idx, run):
    r = np.arange(len(x))
    return x[r[:, None], idx[r % (8 * run) // run]]


E2M1 = np.array([0.0, 0.5, 1.0, 1.5, 2.0, 3.0, 4.0, 6.0, -0.0, -0.5, -1.0, -1.5, -2.0, -3.0, -4.0, -6.0])


def pack_weight(w, fmt):
    k, n = w.shape
    w = f64(np.asarray(w, np.float32).astype(ml_dtypes.bfloat16)).reshape(k // 32, 32, n)
    amax = np.abs(w).max(1)
    if fmt == "e4m3":
        byte = np.frexp(amax)[1] - 1 + 127 - 7
    else:
        mant, ex = np.frexp(amax / 6.0)
        byte = np.where(mant > 0.5, ex, ex - 1) + 127
    byte = np.clip(np.where(amax > 0, byte, 1), 1, 254)
    scaled = (w * np.exp2(127.0 - byte)[:, None, :]).reshape(k, n).astype(np.float32)
    by_word = np.ascontiguousarray(scaled.reshape(k // 512, 128, 4, n).transpose(0, 1, 3, 2))
    if fmt == "e4m3":
        words = by_word.astype(ml_dtypes.float8_e4m3fn).view(np.uint8)
    else:
        c = by_word.astype(ml_dtypes.float4_e2m1fn).view(np.uint8) & 0xF
        words = (c[..., 0::2] | (c[..., 1::2] << 4)).reshape(k // 512, 128, 2 * n)
    return np.ascontiguousarray(words), np.ascontiguousarray(byte.astype(np.uint8).reshape(k // 512, 16, n))


def unpack_weight(words, scales, fmt):
    g, _, n = scales.shape
    words = np.ascontiguousarray(words).reshape(g, 128, n, -1)
    if fmt == "e4m3":
        vals = words.view(ml_dtypes.float8_e4m3fn).astype(np.float64)
    else:
        nib = np.empty((g, 128, n, 4), np.uint8)
        nib[..., 0::2] = words & 0xF
        nib[..., 1::2] = words >> 4
        vals = E2M1[nib]
    vals = vals * np.repeat(np.exp2(scales.astype(np.float64) - 127.0), 8, axis=1)[..., None]
    return vals.transpose(0, 1, 3, 2).reshape(g * 512, n)


K, R, F, T, J, U = 512, 128, 512, 2048, 512, 1024


def setup_inputs():
    n = np.random.standard_normal
    idx = np.random.permutation(T)[:J]
    idx2 = np.stack([np.random.permutation(U)[:J] for _ in range(8)])
    idx3 = np.stack([np.random.permutation(U)[:J] for _ in range(8)])
    fk = mx_kscale(K)
    ff = mx_kscale(F)
    tabp = pack_weight(n((K, T)) / fk[:, None], "e4m3")
    return {
        "tab_words": tabp[0],
        "tab_scales": tabp[1],
        "w1": (n((K, R)) * 1 / np.sqrt(K) * fk[:, None]).astype(np.float32),
        "gain": (np.random.uniform(0.5, 1.5, (R, 1))).astype(np.float32),
        "ground": (n((R, U)) * 0.7).astype(np.float32),
        "wo": (n((F, R)) * 1 / np.sqrt(F) * ff[:, None]).astype(np.float32),
        "dy": (n((F, U)) / ff[:, None]).astype(np.float32),
        "old": (0.5 * n((R, J))).astype(np.float32),
        "offs": striped(idx),
        "offs2": striped8(idx2),
        "offs3": striped8(idx3),
    }


def reference(tab_words, tab_scales, w1, gain, ground, wo, dy, old, offs, offs2, offs3):
    idx = unstriped(offs)
    idx2 = unstriped8(offs2)
    idx3 = unstriped8(offs3)
    tabu = unpack_weight(tab_words, tab_scales, "e4m3")
    w1q = mxq(f64(w1), 0, "e4m3")
    tabidxg = tabu[:, idx]
    a = w1q.T @ tabidxg
    h1 = a * f64(gain)
    pa = np.zeros((R, U))
    pa[np.arange(R)[:, None], idx2[np.arange(R) % 128 // 16]] = h1
    pb = np.zeros((R, U))
    pb[np.arange(R)[:, None], idx3[np.arange(R) % 128 // 16]] = a
    woq = mxq(f64(wo), 0, "e4m3")
    dyq = mxq(f64(dy), 0, "e4m3")
    c0 = woq.T @ dyq
    dpb = c0 * np.tanh(pa + f64(ground))
    dpa = c0 * (pb + f64(ground)) * (1.0 - np.square(np.tanh(pa + f64(ground))))
    dh1 = pick8(dpa, idx2, 16)
    da = pick8(dpb, idx3, 16) + dh1 * f64(gain)
    y = da + f64(old)
    return y

@@ -1,0 +1,159 @@
+from contextlib import ExitStack
+
+import concourse.mybir as mybir
+
+F32 = mybir.dt.float32
+BF16 = mybir.dt.bfloat16
+I32 = mybir.dt.int32
+U32 = mybir.dt.uint32
+U16 = mybir.dt.uint16
+U8 = mybir.dt.uint8
+FP8X4 = mybir.dt.float8_e4m3fn_x4
+ALU = mybir.AluOpType
+ACT = mybir.ActivationFunctionType
+
+P = 128
+PACK = 4
+K, R, F, T, J, U = 512, 128, 512, 2048, 512, 1024
+FLOPS = 2 * K * R * J + 2 * F * R * U
+SLOT_HALF = J // 2
+PAGE_HALF = U // 2
+LIST_COLS = J // 16
+
+
+def tile_attend_ctwopages_kernel(tc, tab_words, tab_scales, w1, gain, ground, wo, dy, old, offs, offs2, offs3, out):
+    nc = tc.nc
+
+    with ExitStack() as ctx:
+        lists = ctx.enter_context(tc.tile_pool(name="lists", bufs=1))
+        sb = ctx.enter_context(tc.tile_pool(name="sb", bufs=1))
+        psum = ctx.enter_context(tc.psum_pool(name="psum", bufs=1))
+
+        def half_list(tile, h):
+            return tile[:, h * (LIST_COLS // 2) : (h + 1) * (LIST_COLS // 2)]
+
+        def interleave(dst, src):
+            nc.scalar.activation(
+                dst[:].rearrange("p (c i t) -> p c t i", i=4, t=PACK),
+                src[:].rearrange("p t (c i) -> p c t i", i=4),
+                ACT.Copy,
+            )
+
+        def quantise(name, grouped, width):
+            codes = sb.tile([P, width], U32, name=name + "_codes", align_bytes=64)
+            scales = sb.tile([P, width], U8, name=name + "_scales", align_bytes=64)
+            nc.vector.quantize_mx(out=codes[:].bitcast(FP8X4), scales=scales[:], in_=grouped[:])
+            return codes[:], scales[:]
+
+        def mx_product(name, lhs, rhs, width):
+            bank = psum.tile([P, width], F32, name=name)
+            nc.tensor.matmul_mx(
+                out=bank[:],
+                lhsT=lhs[0].bitcast(FP8X4),
+                lhsT_scale=lhs[1],
+                rhs=rhs[0].bitcast(FP8X4),
+                rhs_scale=rhs[1],
+                start=True,
+                stop=True,
+            )
+            return bank
+
+        offs_sb = lists.tile([P, LIST_COLS], U16, name="offs_sb")
+        offs2_sb = lists.tile([P, LIST_COLS], U16, name="offs2_sb")
+        offs3_sb = lists.tile([P, LIST_COLS], U16, name="offs3_sb")
+        tab_codes = sb.tile([P, T], U32, name="tab_codes")
+        tab_bytes = sb.tile([P, T], U8, name="tab_bytes")
+        w1_raw = sb.tile([P, PACK, R], F32, name="w1_raw")
+        wo_raw = sb.tile([P, PACK, R], F32, name="wo_raw")
+        dy_raw = [sb.tile([P, PACK, PAGE_HALF], F32, name=f"dy_raw{h}") for h in range(2)]
+        gain_sb = sb.tile([P, 1], F32, name="gain_sb")
+        ground_sb = sb.tile([P, U], F32, name="ground_sb")
+        old_sb = sb.tile([P, J], F32, name="old_sb")
+        page_a = sb.tile([P, U], F32, name="page_a")
+        page_b = sb.tile([P, U], F32, name="page_b")
+
+        nc.gpsimd.memset(tab_bytes[:].bitcast(I32), 0)
+        nc.vector.memset(page_a[:], 0.0)
+        nc.vector.memset(page_b[:], 0.0)
+
+        nc.sync.dma_start(w1_raw[:], w1.rearrange("(p t) r -> p t r", t=PACK))
+        nc.sync.dma_start(offs_sb[:], offs)
+        nc.gpsimd.dma_start(gain_sb[:], gain)
+        for q in range(4):
+            nc.sync.dma_start(
+                tab_bytes[32 * q : 32 * q + 4, :].bitcast(I32), tab_scales[0, 4 * q : 4 * q + 4, :].bitcast(I32)
+            )
+        nc.sync.dma_start(tab_codes[:].bitcast(I32), tab_words[0].rearrange("p n t -> p (n t)").bitcast(I32))
+        nc.sync.dma_start(offs2_sb[:], offs2)
+        nc.sync.dma_start(dy_raw[0][:], dy[:, 0:PAGE_HALF].rearrange("(p t) u -> p t u", t=PACK))
+        nc.sync.dma_start(offs3_sb[:], offs3)
+        nc.sync.dma_start(wo_raw[:], wo.rearrange("(p t) r -> p t r", t=PACK))
+        nc.sync.dma_start(dy_raw[1][:], dy[:, PAGE_HALF:U].rearrange("(p t) u -> p t u", t=PACK))
+        nc.sync.dma_start(ground_sb[:], ground)
+        nc.sync.dma_start(old_sb[:], old)
+
+        w1_bf = sb.tile([P, R * PACK], BF16, name="w1_bf", align_bytes=64)
+        interleave(w1_bf, w1_raw)
+
+        w1_mx = quantise("w1", w1_bf, R)
+        picked_scales = sb.tile([P, J], U8, name="picked_scales", align_bytes=64)
+        nc.vector.tensor_copy(picked_scales[:], tab_bytes[:].indirect(offs_sb[:]))
+        picked = []
+        for h in range(2):
+            codes = sb.tile([P, SLOT_HALF], U32, name=f"picked_codes{h}", align_bytes=64)
+            nc.vector.tensor_copy(codes[:], tab_codes[:].indirect(half_list(offs_sb, h)))
+            picked.append((codes[:], picked_scales[:, h * SLOT_HALF : (h + 1) * SLOT_HALF]))
+
+        a_sb = sb.tile([P, J], F32, name="a_sb")
+        for h in range(2):
+            a_bank = mx_product(f"a_bank{h}", w1_mx, picked[h], SLOT_HALF)
+            h1 = sb.tile([P, SLOT_HALF], F32, name=f"h1_{h}")
+            nc.scalar.activation(h1[:], a_bank[:], ACT.Copy, scale=gain_sb[:])
+            nc.scalar.activation(a_sb[:, h * SLOT_HALF : (h + 1) * SLOT_HALF], a_bank[:], ACT.Copy)
+            nc.vector.tensor_copy(page_a[:].indirect(half_list(offs2_sb, h)), h1[:])
+        nc.vector.tensor_copy(page_b[:].indirect(offs3_sb[:]), a_sb[:])
+
+        dy_bf0 = sb.tile([P, PAGE_HALF * PACK], BF16, name="dy_bf0", align_bytes=64)
+        interleave(dy_bf0, dy_raw[0])
+        wo_bf = sb.tile([P, R * PACK], BF16, name="wo_bf", align_bytes=64)
+        interleave(wo_bf, wo_raw)
+        dy_bf1 = sb.tile([P, PAGE_HALF * PACK], BF16, name="dy_bf1", tag="dy_bf1", align_bytes=64)
+        interleave(dy_bf1, dy_raw[1])
+        wo_mx = quantise("wo", wo_bf, R)
+        c0 = []
+        for h, dy_bf in enumerate((dy_bf0, dy_bf1)):
+            dy_mx = quantise(f"dy{h}", dy_bf, PAGE_HALF)
+            c0.append(mx_product(f"c0_bank{h}", wo_mx, dy_mx, PAGE_HALF))
+
+        halves = [slice(h * PAGE_HALF, (h + 1) * PAGE_HALF) for h in range(2)]
+        z = [sb.tile([P, PAGE_HALF], F32, name=f"z{h}") for h in range(2)]
+        for h in range(2):
+            nc.gpsimd.tensor_tensor(z[h][:], page_a[:, halves[h]], ground_sb[:, halves[h]], ALU.add)
+        tanh_z = [dy_raw[1][:, h, :] for h in range(2)]
+        tanh_sq = [dy_raw[1][:, 2 + h, :] for h in range(2)]
+        for h in range(2):
+            nc.scalar.activation(tanh_z[h], z[h][:], ACT.Tanh)
+            nc.scalar.activation(tanh_sq[h], tanh_z[h], ACT.Square)
+
+        second = sb.tile([P, U], F32, name="second", tag="dy_bf1", align_bytes=64)
+        for h in range(2):
+            nc.gpsimd.tensor_tensor(second[:, halves[h]], page_b[:, halves[h]], ground_sb[:, halves[h]], ALU.add)
+
+        dpb = sb.tile([P, U], F32, name="dpb")
+        neg_slope = sb.tile([P, U], F32, name="neg_slope")
+        for h in range(2):
+            nc.vector.tensor_tensor(dpb[:, halves[h]], c0[h][:], tanh_z[h], ALU.mult)
+            nc.vector.scalar_tensor_tensor(neg_slope[:, halves[h]], tanh_sq[h], 1.0, c0[h][:], ALU.subtract, ALU.mult)
+        from_b = sb.tile([P, J], F32, name="from_b")
+        nc.vector.tensor_tensor(from_b[:], dpb[:].indirect(offs3_sb[:]), old_sb[:], ALU.add)
+        dpa = sb.tile([P, U], F32, name="dpa")
+        nc.vector.scalar_tensor_tensor(dpa[:], neg_slope[:], -1.0, second[:], ALU.mult, ALU.mult)
+
+        dh1 = [sb.tile([P, SLOT_HALF], F32, name=f"dh1_{h}") for h in range(2)]
+        for h in range(2):
+            nc.vector.tensor_copy(dh1[h][:], dpa[:].indirect(half_list(offs2_sb, h)))
+        for h, queue in enumerate((nc.sync, nc.scalar)):
+            slots = slice(h * SLOT_HALF, (h + 1) * SLOT_HALF)
+            result = sb.tile([P, SLOT_HALF], F32, name=f"result{h}")
+            nc.vector.scalar_tensor_tensor(result[:], dh1[h][:], gain_sb[:], from_b[:, slots], ALU.mult, ALU.add)
+            queue.dma_start(out[:, slots], result[:])

@@ -1,6 +1,7 @@
 from contextlib import ExitStack
 
 import concourse.mybir as mybir
+from concourse.masks import make_identity
 
 F32 = mybir.dt.float32
 BF16 = mybir.dt.bfloat16
@@ -19,6 +20,7 @@ FLOPS = 2 * K * R * J + 2 * F * R * U
 SLOT_HALF = J // 2
 PAGE_HALF = U // 2
 LIST_COLS = J // 16
+BLOCKS = PAGE_HALF // P
 
 
 def tile_attend_ctwopages_kernel(tc, tab_words, tab_scales, w1, gain, ground, wo, dy, old, offs, offs2, offs3, out):
@@ -45,10 +47,26 @@ def tile_attend_ctwopages_kernel(tc, tab_words, tab_scales, w1, gain, ground, wo
             nc.vector.quantize_mx(out=codes[:].bitcast(FP8X4), scales=scales[:], in_=grouped[:])
             return codes[:], scales[:]
 
-        def mx_product(name, lhs, rhs, width):
-            bank = psum.tile([P, width], F32, name=name)
+        def bank_tile(name, tag):
+            return psum.tile([P, PAGE_HALF], F32, name=name, tag=tag)
+
+        def block(b):
+            return slice(b * P, (b + 1) * P)
+
+        def turn(bank, src, first, last):
+            for b in range(BLOCKS):
+                nc.tensor.matmul(
+                    bank[:, block(b)],
+                    src[:, block(b)],
+                    identity[:],
+                    start=first and b == 0,
+                    stop=last and b == BLOCKS - 1,
+                    is_transpose=True,
+                )
+
+        def mx_product(dst, lhs, rhs):
             nc.tensor.matmul_mx(
-                out=bank[:],
+                out=dst,
                 lhsT=lhs[0].bitcast(FP8X4),
                 lhsT_scale=lhs[1],
                 rhs=rhs[0].bitcast(FP8X4),
@@ -56,7 +74,6 @@ def tile_attend_ctwopages_kernel(tc, tab_words, tab_scales, w1, gain, ground, wo
                 start=True,
                 stop=True,
             )
-            return bank
 
         offs_sb = lists.tile([P, LIST_COLS], U16, name="offs_sb")
         offs2_sb = lists.tile([P, LIST_COLS], U16, name="offs2_sb")
@@ -79,15 +96,17 @@ def tile_attend_ctwopages_kernel(tc, tab_words, tab_scales, w1, gain, ground, wo
         nc.sync.dma_start(w1_raw[:], w1.rearrange("(p t) r -> p t r", t=PACK))
         nc.sync.dma_start(offs_sb[:], offs)
         nc.gpsimd.dma_start(gain_sb[:], gain)
+        identity = sb.tile([P, P], F32, name="identity")
+        make_identity(nc, identity[:])
         for q in range(4):
             nc.sync.dma_start(
                 tab_bytes[32 * q : 32 * q + 4, :].bitcast(I32), tab_scales[0, 4 * q : 4 * q + 4, :].bitcast(I32)
             )
         nc.sync.dma_start(tab_codes[:].bitcast(I32), tab_words[0].rearrange("p n t -> p (n t)").bitcast(I32))
+        nc.sync.dma_start(wo_raw[:], wo.rearrange("(p t) r -> p t r", t=PACK))
         nc.sync.dma_start(offs2_sb[:], offs2)
         nc.sync.dma_start(dy_raw[0][:], dy[:, 0:PAGE_HALF].rearrange("(p t) u -> p t u", t=PACK))
         nc.sync.dma_start(offs3_sb[:], offs3)
-        nc.sync.dma_start(wo_raw[:], wo.rearrange("(p t) r -> p t r", t=PACK))
         nc.sync.dma_start(dy_raw[1][:], dy[:, PAGE_HALF:U].rearrange("(p t) u -> p t u", t=PACK))
         nc.sync.dma_start(ground_sb[:], ground)
         nc.sync.dma_start(old_sb[:], old)
@@ -104,56 +123,78 @@ def tile_attend_ctwopages_kernel(tc, tab_words, tab_scales, w1, gain, ground, wo
             nc.vector.tensor_copy(codes[:], tab_codes[:].indirect(half_list(offs_sb, h)))
             picked.append((codes[:], picked_scales[:, h * SLOT_HALF : (h + 1) * SLOT_HALF]))
 
+        wo_bf = sb.tile([P, R * PACK], BF16, name="wo_bf", align_bytes=64)
+        interleave(wo_bf, wo_raw)
+        wo_mx = quantise("wo", wo_bf, R)
+
         a_sb = sb.tile([P, J], F32, name="a_sb")
         for h in range(2):
-            a_bank = mx_product(f"a_bank{h}", w1_mx, picked[h], SLOT_HALF)
+            a_bank = bank_tile(f"a_bank{h}", f"slots{h}")
+            mx_product(a_bank[:, 0:SLOT_HALF], w1_mx, picked[h])
             h1 = sb.tile([P, SLOT_HALF], F32, name=f"h1_{h}")
-            nc.scalar.activation(h1[:], a_bank[:], ACT.Copy, scale=gain_sb[:])
-            nc.scalar.activation(a_sb[:, h * SLOT_HALF : (h + 1) * SLOT_HALF], a_bank[:], ACT.Copy)
+            nc.scalar.activation(h1[:], a_bank[:, 0:SLOT_HALF], ACT.Copy, scale=gain_sb[:])
+            nc.scalar.activation(a_sb[:, h * SLOT_HALF : (h + 1) * SLOT_HALF], a_bank[:, 0:SLOT_HALF], ACT.Copy)
             nc.vector.tensor_copy(page_a[:].indirect(half_list(offs2_sb, h)), h1[:])
         nc.vector.tensor_copy(page_b[:].indirect(offs3_sb[:]), a_sb[:])
 
-        dy_bf0 = sb.tile([P, PAGE_HALF * PACK], BF16, name="dy_bf0", align_bytes=64)
-        interleave(dy_bf0, dy_raw[0])
-        wo_bf = sb.tile([P, R * PACK], BF16, name="wo_bf", align_bytes=64)
-        interleave(wo_bf, wo_raw)
-        dy_bf1 = sb.tile([P, PAGE_HALF * PACK], BF16, name="dy_bf1", tag="dy_bf1", align_bytes=64)
-        interleave(dy_bf1, dy_raw[1])
-        wo_mx = quantise("wo", wo_bf, R)
-        c0 = []
-        for h, dy_bf in enumerate((dy_bf0, dy_bf1)):
-            dy_mx = quantise(f"dy{h}", dy_bf, PAGE_HALF)
-            c0.append(mx_product(f"c0_bank{h}", wo_mx, dy_mx, PAGE_HALF))
-
         halves = [slice(h * PAGE_HALF, (h + 1) * PAGE_HALF) for h in range(2)]
-        z = [sb.tile([P, PAGE_HALF], F32, name=f"z{h}") for h in range(2)]
+        z = [bank_tile(f"z{h}", f"z{h}") for h in range(2)]
         for h in range(2):
-            nc.gpsimd.tensor_tensor(z[h][:], page_a[:, halves[h]], ground_sb[:, halves[h]], ALU.add)
+            turn(z[h], page_a[:, halves[h]], True, False)
+        for h in range(2):
+            turn(z[h], ground_sb[:, halves[h]], False, True)
+
+        dy_mx = []
+        for h in range(2):
+            dy_bf = sb.tile([P, PAGE_HALF * PACK], BF16, name=f"dy_bf{h}", align_bytes=64)
+            interleave(dy_bf, dy_raw[h])
+            dy_mx.append(quantise(f"dy{h}", dy_bf, PAGE_HALF))
+
         tanh_z = [dy_raw[1][:, h, :] for h in range(2)]
         tanh_sq = [dy_raw[1][:, 2 + h, :] for h in range(2)]
         for h in range(2):
             nc.scalar.activation(tanh_z[h], z[h][:], ACT.Tanh)
             nc.scalar.activation(tanh_sq[h], tanh_z[h], ACT.Square)
 
-        second = sb.tile([P, U], F32, name="second", tag="dy_bf1", align_bytes=64)
+        c0 = [bank_tile("c0_0", "z0"), bank_tile("c0_1", "c0_1")]
         for h in range(2):
-            nc.gpsimd.tensor_tensor(second[:, halves[h]], page_b[:, halves[h]], ground_sb[:, halves[h]], ALU.add)
+            codes, scales = dy_mx[h]
+            for b in range(BLOCKS):
+                mx_product(c0[h][:, block(b)], (codes[:, block(b)], scales[:, block(b)]), wo_mx)
+
+        second = [bank_tile("second0", "second0"), bank_tile("second1", "z1")]
+        for h in range(2):
+            turn(second[h], ground_sb[:, halves[h]], True, False)
+            turn(second[h], page_b[:, halves[h]], False, True)
+
+        neg_slope = [sb.tile([P, PAGE_HALF], F32, name=f"neg_slope{h}") for h in range(2)]
+        for h in range(2):
+            nc.vector.scalar_tensor_tensor(neg_slope[h][:], tanh_sq[h], 1.0, c0[h][:], ALU.subtract, ALU.mult)
+
+        dpa = sb.tile([P, U], F32, name="dpa")
+        for h in range(2):
+            dpa_t = sb.tile([P, PAGE_HALF], F32, name=f"dpa_t{h}")
+            nc.vector.scalar_tensor_tensor(dpa_t[:], second[h][:], -1.0, neg_slope[h][:], ALU.mult, ALU.mult)
+            back = bank_tile(f"dpa_back{h}", f"slots{h}")
+            turn(back, dpa_t, True, True)
+            nc.scalar.copy(dpa[:, halves[h]], back[:])
 
         dpb = sb.tile([P, U], F32, name="dpb")
-        neg_slope = sb.tile([P, U], F32, name="neg_slope")
         for h in range(2):
-            nc.vector.tensor_tensor(dpb[:, halves[h]], c0[h][:], tanh_z[h], ALU.mult)
-            nc.vector.scalar_tensor_tensor(neg_slope[:, halves[h]], tanh_sq[h], 1.0, c0[h][:], ALU.subtract, ALU.mult)
-        from_b = sb.tile([P, J], F32, name="from_b")
-        nc.vector.tensor_tensor(from_b[:], dpb[:].indirect(offs3_sb[:]), old_sb[:], ALU.add)
-        dpa = sb.tile([P, U], F32, name="dpa")
-        nc.vector.scalar_tensor_tensor(dpa[:], neg_slope[:], -1.0, second[:], ALU.mult, ALU.mult)
+            dpb_t = sb.tile([P, PAGE_HALF], F32, name=f"dpb_t{h}")
+            nc.vector.tensor_tensor(dpb_t[:], c0[h][:], tanh_z[h], ALU.mult)
+            back = bank_tile(f"dpb_back{h}", f"dpb_back{h}")
+            turn(back, dpb_t, True, True)
+            nc.scalar.copy(dpb[:, halves[h]], back[:])
 
+        slots = [slice(h * SLOT_HALF, (h + 1) * SLOT_HALF) for h in range(2)]
         dh1 = [sb.tile([P, SLOT_HALF], F32, name=f"dh1_{h}") for h in range(2)]
         for h in range(2):
             nc.vector.tensor_copy(dh1[h][:], dpa[:].indirect(half_list(offs2_sb, h)))
+        from_a = [sb.tile([P, SLOT_HALF], F32, name=f"from_a{h}") for h in range(2)]
+        for h in range(2):
+            nc.vector.scalar_tensor_tensor(from_a[h][:], dh1[h][:], gain_sb[:], old_sb[:, slots[h]], ALU.mult, ALU.add)
         for h, queue in enumerate((nc.sync, nc.scalar)):
-            slots = slice(h * SLOT_HALF, (h + 1) * SLOT_HALF)
             result = sb.tile([P, SLOT_HALF], F32, name=f"result{h}")
-            nc.vector.scalar_tensor_tensor(result[:], dh1[h][:], gain_sb[:], from_b[:, slots], ALU.mult, ALU.add)
-            queue.dma_start(out[:, slots], result[:])
+            nc.vector.tensor_tensor(result[:], dpb[:].indirect(half_list(offs3_sb, h)), from_a[h][:], ALU.add)
+            queue.dma_start(out[:, slots[h]], result[:])

@@ -53,14 +53,14 @@ def tile_attend_ctwopages_kernel(tc, tab_words, tab_scales, w1, gain, ground, wo
         def block(b):
             return slice(b * P, (b + 1) * P)
 
-        def turn(bank, src, first, last):
-            for b in range(BLOCKS):
+        def turn(bank, src, first, last, blocks=BLOCKS):
+            for b in range(blocks):
                 nc.tensor.matmul(
                     bank[:, block(b)],
                     src[:, block(b)],
                     identity[:],
                     start=first and b == 0,
-                    stop=last and b == BLOCKS - 1,
+                    stop=last and b == blocks - 1,
                     is_transpose=True,
                 )
 
@@ -89,13 +89,12 @@ def tile_attend_ctwopages_kernel(tc, tab_words, tab_scales, w1, gain, ground, wo
         page_a = sb.tile([P, U], F32, name="page_a")
         page_b = sb.tile([P, U], F32, name="page_b")
 
-        nc.gpsimd.memset(tab_bytes[:].bitcast(I32), 0)
+        nc.vector.memset(tab_bytes[:].bitcast(I32), 0)
         nc.vector.memset(page_a[:], 0.0)
         nc.vector.memset(page_b[:], 0.0)
 
         nc.sync.dma_start(w1_raw[:], w1.rearrange("(p t) r -> p t r", t=PACK))
         nc.sync.dma_start(offs_sb[:], offs)
-        nc.gpsimd.dma_start(gain_sb[:], gain)
         identity = sb.tile([P, P], F32, name="identity")
         make_identity(nc, identity[:])
         for q in range(4):
@@ -103,6 +102,7 @@ def tile_attend_ctwopages_kernel(tc, tab_words, tab_scales, w1, gain, ground, wo
                 tab_bytes[32 * q : 32 * q + 4, :].bitcast(I32), tab_scales[0, 4 * q : 4 * q + 4, :].bitcast(I32)
             )
         nc.sync.dma_start(tab_codes[:].bitcast(I32), tab_words[0].rearrange("p n t -> p (n t)").bitcast(I32))
+        nc.sync.dma_start(gain_sb[:], gain)
         nc.sync.dma_start(wo_raw[:], wo.rearrange("(p t) r -> p t r", t=PACK))
         nc.sync.dma_start(offs2_sb[:], offs2)
         nc.sync.dma_start(dy_raw[0][:], dy[:, 0:PAGE_HALF].rearrange("(p t) u -> p t u", t=PACK))
@@ -127,15 +127,17 @@ def tile_attend_ctwopages_kernel(tc, tab_words, tab_scales, w1, gain, ground, wo
         interleave(wo_bf, wo_raw)
         wo_mx = quantise("wo", wo_bf, R)
 
-        a_sb = sb.tile([P, J], F32, name="a_sb")
+        a_banks = []
         for h in range(2):
             a_bank = bank_tile(f"a_bank{h}", f"slots{h}")
             mx_product(a_bank[:, 0:SLOT_HALF], w1_mx, picked[h])
             h1 = sb.tile([P, SLOT_HALF], F32, name=f"h1_{h}")
             nc.scalar.activation(h1[:], a_bank[:, 0:SLOT_HALF], ACT.Copy, scale=gain_sb[:])
-            nc.scalar.activation(a_sb[:, h * SLOT_HALF : (h + 1) * SLOT_HALF], a_bank[:, 0:SLOT_HALF], ACT.Copy)
             nc.vector.tensor_copy(page_a[:].indirect(half_list(offs2_sb, h)), h1[:])
-        nc.vector.tensor_copy(page_b[:].indirect(offs3_sb[:]), a_sb[:])
+            a_banks.append(a_bank)
+        a_first = sb.tile([P, SLOT_HALF], F32, name="a_first")
+        nc.scalar.copy(a_first[:], a_banks[0][:, 0:SLOT_HALF])
+        nc.vector.tensor_copy(page_b[:].indirect(half_list(offs3_sb, 0)), a_first[:])
 
         halves = [slice(h * PAGE_HALF, (h + 1) * PAGE_HALF) for h in range(2)]
         z = [bank_tile(f"z{h}", f"z{h}") for h in range(2)]
@@ -143,58 +145,64 @@ def tile_attend_ctwopages_kernel(tc, tab_words, tab_scales, w1, gain, ground, wo
             turn(z[h], page_a[:, halves[h]], True, False)
         for h in range(2):
             turn(z[h], ground_sb[:, halves[h]], False, True)
+        second = [bank_tile(f"second{h}", f"second{h}") for h in range(2)]
+        for h in range(2):
+            turn(second[h], ground_sb[:, halves[h]], True, False)
 
         dy_mx = []
         for h in range(2):
             dy_bf = sb.tile([P, PAGE_HALF * PACK], BF16, name=f"dy_bf{h}", align_bytes=64)
             interleave(dy_bf, dy_raw[h])
             dy_mx.append(quantise(f"dy{h}", dy_bf, PAGE_HALF))
+            a_late = dy_raw[h][:, 2, 0:P]
+            nc.scalar.copy(a_late, a_banks[1][:, block(h)])
+            cols = LIST_COLS // 4
+            nc.vector.tensor_copy(page_b[:].indirect(offs3_sb[:, (2 + h) * cols : (3 + h) * cols]), a_late)
 
         tanh_z = [dy_raw[1][:, h, :] for h in range(2)]
-        tanh_sq = [dy_raw[1][:, 2 + h, :] for h in range(2)]
+        tanh_sq = [sb.tile([P, PAGE_HALF], F32, name=f"tanh_sq{h}") for h in range(2)]
         for h in range(2):
             nc.scalar.activation(tanh_z[h], z[h][:], ACT.Tanh)
-            nc.scalar.activation(tanh_sq[h], tanh_z[h], ACT.Square)
+        for h in range(2):
+            nc.scalar.activation(tanh_sq[h][:], tanh_z[h], ACT.Square)
 
         c0 = [bank_tile("c0_0", "z0"), bank_tile("c0_1", "c0_1")]
         for h in range(2):
             codes, scales = dy_mx[h]
             for b in range(BLOCKS):
                 mx_product(c0[h][:, block(b)], (codes[:, block(b)], scales[:, block(b)]), wo_mx)
-
-        second = [bank_tile("second0", "second0"), bank_tile("second1", "z1")]
         for h in range(2):
-            turn(second[h], ground_sb[:, halves[h]], True, False)
             turn(second[h], page_b[:, halves[h]], False, True)
-
-        neg_slope = [sb.tile([P, PAGE_HALF], F32, name=f"neg_slope{h}") for h in range(2)]
-        for h in range(2):
-            nc.vector.scalar_tensor_tensor(neg_slope[h][:], tanh_sq[h], 1.0, c0[h][:], ALU.subtract, ALU.mult)
-
-        dpa = sb.tile([P, U], F32, name="dpa")
-        for h in range(2):
-            dpa_t = sb.tile([P, PAGE_HALF], F32, name=f"dpa_t{h}")
-            nc.vector.scalar_tensor_tensor(dpa_t[:], second[h][:], -1.0, neg_slope[h][:], ALU.mult, ALU.mult)
-            back = bank_tile(f"dpa_back{h}", f"slots{h}")
-            turn(back, dpa_t, True, True)
-            nc.scalar.copy(dpa[:, halves[h]], back[:])
 
         dpb = sb.tile([P, U], F32, name="dpb")
         for h in range(2):
             dpb_t = sb.tile([P, PAGE_HALF], F32, name=f"dpb_t{h}")
             nc.vector.tensor_tensor(dpb_t[:], c0[h][:], tanh_z[h], ALU.mult)
-            back = bank_tile(f"dpb_back{h}", f"dpb_back{h}")
-            turn(back, dpb_t, True, True)
+            back = bank_tile(f"dpb_back{h}", ("z1", "dpb_back")[h])
+            turn(back, dpb_t[:], True, True)
             nc.scalar.copy(dpb[:, halves[h]], back[:])
 
-        slots = [slice(h * SLOT_HALF, (h + 1) * SLOT_HALF) for h in range(2)]
+        neg_slope = [sb.tile([P, PAGE_HALF], F32, name=f"neg_slope{h}") for h in range(2)]
+        for h in range(2):
+            nc.vector.scalar_tensor_tensor(neg_slope[h][:], tanh_sq[h][:], 1.0, c0[h][:], ALU.subtract, ALU.mult)
+
+        dpa = sb.tile([P, U], F32, name="dpa")
+        for h in range(2):
+            dpa_t = sb.tile([P, PAGE_HALF], F32, name=f"dpa_t{h}")
+            nc.vector.scalar_tensor_tensor(dpa_t[:], second[h][:], -1.0, neg_slope[h][:], ALU.mult, ALU.mult)
+            for g in range(2):
+                back = bank_tile(f"dpa_back{h}{g}", (("slots0", "slots1"), ("z0", "c0_1"))[h][g])
+                turn(back, dpa_t[:, g * SLOT_HALF : (g + 1) * SLOT_HALF], True, True, 2)
+                start = h * PAGE_HALF + g * SLOT_HALF
+                nc.scalar.copy(dpa[:, start : start + SLOT_HALF], back[:, 0:SLOT_HALF])
+
+        from_b = sb.tile([P, J], F32, name="from_b")
+        nc.vector.tensor_tensor(from_b[:], dpb[:].indirect(offs3_sb[:]), old_sb[:], ALU.add)
         dh1 = [sb.tile([P, SLOT_HALF], F32, name=f"dh1_{h}") for h in range(2)]
         for h in range(2):
             nc.vector.tensor_copy(dh1[h][:], dpa[:].indirect(half_list(offs2_sb, h)))
-        from_a = [sb.tile([P, SLOT_HALF], F32, name=f"from_a{h}") for h in range(2)]
-        for h in range(2):
-            nc.vector.scalar_tensor_tensor(from_a[h][:], dh1[h][:], gain_sb[:], old_sb[:, slots[h]], ALU.mult, ALU.add)
         for h, queue in enumerate((nc.sync, nc.scalar)):
+            slots = slice(h * SLOT_HALF, (h + 1) * SLOT_HALF)
             result = sb.tile([P, SLOT_HALF], F32, name=f"result{h}")
-            nc.vector.tensor_tensor(result[:], dpb[:].indirect(half_list(offs3_sb, h)), from_a[h][:], ALU.add)
-            queue.dma_start(out[:, slots[h]], result[:])
+            nc.vector.scalar_tensor_tensor(result[:], dh1[h][:], gain_sb[:], from_b[:, slots], ALU.mult, ALU.add)
+            queue.dma_start(out[:, slots], result[:])

from contextlib import ExitStack

import concourse.mybir as mybir
from concourse.masks import make_identity

F32 = mybir.dt.float32
BF16 = mybir.dt.bfloat16
I32 = mybir.dt.int32
U32 = mybir.dt.uint32
U16 = mybir.dt.uint16
U8 = mybir.dt.uint8
FP8X4 = mybir.dt.float8_e4m3fn_x4
ALU = mybir.AluOpType
ACT = mybir.ActivationFunctionType

P = 128
PACK = 4
K, R, F, T, J, U = 512, 128, 512, 2048, 512, 1024
FLOPS = 2 * K * R * J + 2 * F * R * U
SLOT_HALF = J // 2
PAGE_HALF = U // 2
LIST_COLS = J // 16
BLOCKS = PAGE_HALF // P


def tile_attend_ctwopages_kernel(tc, tab_words, tab_scales, w1, gain, ground, wo, dy, old, offs, offs2, offs3, out):
    nc = tc.nc

    with ExitStack() as ctx:
        lists = ctx.enter_context(tc.tile_pool(name="lists", bufs=1))
        sb = ctx.enter_context(tc.tile_pool(name="sb", bufs=1))
        psum = ctx.enter_context(tc.psum_pool(name="psum", bufs=1))

        def half_list(tile, h):
            return tile[:, h * (LIST_COLS // 2) : (h + 1) * (LIST_COLS // 2)]

        def interleave(dst, src):
            nc.scalar.activation(
                dst[:].rearrange("p (c i t) -> p c t i", i=4, t=PACK),
                src[:].rearrange("p t (c i) -> p c t i", i=4),
                ACT.Copy,
            )

        def quantise(name, grouped, width):
            codes = sb.tile([P, width], U32, name=name + "_codes", align_bytes=64)
            scales = sb.tile([P, width], U8, name=name + "_scales", align_bytes=64)
            nc.vector.quantize_mx(out=codes[:].bitcast(FP8X4), scales=scales[:], in_=grouped[:])
            return codes[:], scales[:]

        def bank_tile(name, tag):
            return psum.tile([P, PAGE_HALF], F32, name=name, tag=tag)

        def block(b):
            return slice(b * P, (b + 1) * P)

        def turn(bank, src, first, last, blocks=BLOCKS):
            for b in range(blocks):
                nc.tensor.matmul(
                    bank[:, block(b)],
                    src[:, block(b)],
                    identity[:],
                    start=first and b == 0,
                    stop=last and b == blocks - 1,
                    is_transpose=True,
                )

        def mx_product(dst, lhs, rhs):
            nc.tensor.matmul_mx(
                out=dst,
                lhsT=lhs[0].bitcast(FP8X4),
                lhsT_scale=lhs[1],
                rhs=rhs[0].bitcast(FP8X4),
                rhs_scale=rhs[1],
                start=True,
                stop=True,
            )

        offs_sb = lists.tile([P, LIST_COLS], U16, name="offs_sb")
        offs2_sb = lists.tile([P, LIST_COLS], U16, name="offs2_sb")
        offs3_sb = lists.tile([P, LIST_COLS], U16, name="offs3_sb")
        tab_codes = sb.tile([P, T], U32, name="tab_codes")
        tab_bytes = sb.tile([P, T], U8, name="tab_bytes")
        w1_raw = sb.tile([P, PACK, R], F32, name="w1_raw")
        wo_raw = sb.tile([P, PACK, R], F32, name="wo_raw")
        dy_raw = [sb.tile([P, PACK, PAGE_HALF], F32, name=f"dy_raw{h}") for h in range(2)]
        gain_sb = sb.tile([P, 1], F32, name="gain_sb")
        ground_sb = sb.tile([P, U], F32, name="ground_sb")
        old_sb = sb.tile([P, J], F32, name="old_sb")
        page_a = sb.tile([P, U], F32, name="page_a")
        page_b = sb.tile([P, U], F32, name="page_b")

        nc.vector.memset(tab_bytes[:].bitcast(I32), 0)
        nc.vector.memset(page_a[:], 0.0)
        nc.vector.memset(page_b[:], 0.0)

        nc.sync.dma_start(w1_raw[:], w1.rearrange("(p t) r -> p t r", t=PACK))
        nc.sync.dma_start(offs_sb[:], offs)
        identity = sb.tile([P, P], F32, name="identity")
        make_identity(nc, identity[:])
        for q in range(4):
            nc.sync.dma_start(
                tab_bytes[32 * q : 32 * q + 4, :].bitcast(I32), tab_scales[0, 4 * q : 4 * q + 4, :].bitcast(I32)
            )
        nc.sync.dma_start(tab_codes[:].bitcast(I32), tab_words[0].rearrange("p n t -> p (n t)").bitcast(I32))
        nc.sync.dma_start(gain_sb[:], gain)
        nc.sync.dma_start(wo_raw[:], wo.rearrange("(p t) r -> p t r", t=PACK))
        nc.sync.dma_start(offs2_sb[:], offs2)
        nc.sync.dma_start(dy_raw[0][:], dy[:, 0:PAGE_HALF].rearrange("(p t) u -> p t u", t=PACK))
        nc.sync.dma_start(offs3_sb[:], offs3)
        nc.sync.dma_start(dy_raw[1][:], dy[:, PAGE_HALF:U].rearrange("(p t) u -> p t u", t=PACK))
        nc.sync.dma_start(ground_sb[:], ground)
        nc.sync.dma_start(old_sb[:], old)

        w1_bf = sb.tile([P, R * PACK], BF16, name="w1_bf", align_bytes=64)
        interleave(w1_bf, w1_raw)

        w1_mx = quantise("w1", w1_bf, R)
        picked_scales = sb.tile([P, J], U8, name="picked_scales", align_bytes=64)
        nc.vector.tensor_copy(picked_scales[:], tab_bytes[:].indirect(offs_sb[:]))
        picked = []
        for h in range(2):
            codes = sb.tile([P, SLOT_HALF], U32, name=f"picked_codes{h}", align_bytes=64)
            nc.vector.tensor_copy(codes[:], tab_codes[:].indirect(half_list(offs_sb, h)))
            picked.append((codes[:], picked_scales[:, h * SLOT_HALF : (h + 1) * SLOT_HALF]))

        wo_bf = sb.tile([P, R * PACK], BF16, name="wo_bf", align_bytes=64)
        interleave(wo_bf, wo_raw)
        wo_mx = quantise("wo", wo_bf, R)

        a_banks = []
        for h in range(2):
            a_bank = bank_tile(f"a_bank{h}", f"slots{h}")
            mx_product(a_bank[:, 0:SLOT_HALF], w1_mx, picked[h])
            h1 = sb.tile([P, SLOT_HALF], F32, name=f"h1_{h}")
            nc.scalar.activation(h1[:], a_bank[:, 0:SLOT_HALF], ACT.Copy, scale=gain_sb[:])
            nc.vector.tensor_copy(page_a[:].indirect(half_list(offs2_sb, h)), h1[:])
            a_banks.append(a_bank)
        a_first = sb.tile([P, SLOT_HALF], F32, name="a_first")
        nc.scalar.copy(a_first[:], a_banks[0][:, 0:SLOT_HALF])
        nc.vector.tensor_copy(page_b[:].indirect(half_list(offs3_sb, 0)), a_first[:])

        halves = [slice(h * PAGE_HALF, (h + 1) * PAGE_HALF) for h in range(2)]
        z = [bank_tile(f"z{h}", f"z{h}") for h in range(2)]
        for h in range(2):
            turn(z[h], page_a[:, halves[h]], True, False)
        for h in range(2):
            turn(z[h], ground_sb[:, halves[h]], False, True)
        second = [bank_tile(f"second{h}", f"second{h}") for h in range(2)]
        for h in range(2):
            turn(second[h], ground_sb[:, halves[h]], True, False)

        dy_mx = []
        for h in range(2):
            dy_bf = sb.tile([P, PAGE_HALF * PACK], BF16, name=f"dy_bf{h}", align_bytes=64)
            interleave(dy_bf, dy_raw[h])
            dy_mx.append(quantise(f"dy{h}", dy_bf, PAGE_HALF))
            a_late = dy_raw[h][:, 2, 0:P]
            nc.scalar.copy(a_late, a_banks[1][:, block(h)])
            cols = LIST_COLS // 4
            nc.vector.tensor_copy(page_b[:].indirect(offs3_sb[:, (2 + h) * cols : (3 + h) * cols]), a_late)

        tanh_z = [dy_raw[1][:, h, :] for h in range(2)]
        tanh_sq = [sb.tile([P, PAGE_HALF], F32, name=f"tanh_sq{h}") for h in range(2)]
        for h in range(2):
            nc.scalar.activation(tanh_z[h], z[h][:], ACT.Tanh)
        for h in range(2):
            nc.scalar.activation(tanh_sq[h][:], tanh_z[h], ACT.Square)

        c0 = [bank_tile("c0_0", "z0"), bank_tile("c0_1", "c0_1")]
        for h in range(2):
            codes, scales = dy_mx[h]
            for b in range(BLOCKS):
                mx_product(c0[h][:, block(b)], (codes[:, block(b)], scales[:, block(b)]), wo_mx)
        for h in range(2):
            turn(second[h], page_b[:, halves[h]], False, True)

        dpb = sb.tile([P, U], F32, name="dpb")
        for h in range(2):
            dpb_t = sb.tile([P, PAGE_HALF], F32, name=f"dpb_t{h}")
            nc.vector.tensor_tensor(dpb_t[:], c0[h][:], tanh_z[h], ALU.mult)
            back = bank_tile(f"dpb_back{h}", ("z1", "dpb_back")[h])
            turn(back, dpb_t[:], True, True)
            nc.scalar.copy(dpb[:, halves[h]], back[:])

        neg_slope = [sb.tile([P, PAGE_HALF], F32, name=f"neg_slope{h}") for h in range(2)]
        for h in range(2):
            nc.vector.scalar_tensor_tensor(neg_slope[h][:], tanh_sq[h][:], 1.0, c0[h][:], ALU.subtract, ALU.mult)

        dpa = sb.tile([P, U], F32, name="dpa")
        for h in range(2):
            dpa_t = sb.tile([P, PAGE_HALF], F32, name=f"dpa_t{h}")
            nc.vector.scalar_tensor_tensor(dpa_t[:], second[h][:], -1.0, neg_slope[h][:], ALU.mult, ALU.mult)
            for g in range(2):
                back = bank_tile(f"dpa_back{h}{g}", (("slots0", "slots1"), ("z0", "c0_1"))[h][g])
                turn(back, dpa_t[:, g * SLOT_HALF : (g + 1) * SLOT_HALF], True, True, 2)
                start = h * PAGE_HALF + g * SLOT_HALF
                nc.scalar.copy(dpa[:, start : start + SLOT_HALF], back[:, 0:SLOT_HALF])

        from_b = sb.tile([P, J], F32, name="from_b")
        nc.vector.tensor_tensor(from_b[:], dpb[:].indirect(offs3_sb[:]), old_sb[:], ALU.add)
        dh1 = [sb.tile([P, SLOT_HALF], F32, name=f"dh1_{h}") for h in range(2)]
        for h in range(2):
            nc.vector.tensor_copy(dh1[h][:], dpa[:].indirect(half_list(offs2_sb, h)))
        for h, queue in enumerate((nc.sync, nc.scalar)):
            slots = slice(h * SLOT_HALF, (h + 1) * SLOT_HALF)
            result = sb.tile([P, SLOT_HALF], F32, name=f"result{h}")
            nc.vector.scalar_tensor_tensor(result[:], dh1[h][:], gain_sb[:], from_b[:, slots], ALU.mult, ALU.add)
            queue.dma_start(out[:, slots], result[:])
